import numpy as np
import ml_dtypes


def mxq(x, axis, fmt="e4m3"):
    dtype, down = {"e4m3": (ml_dtypes.float8_e4m3fn, 7), "e5m2": (ml_dtypes.float8_e5m2, 14)}[fmt]
    v = np.moveaxis(np.asarray(x, np.float32).astype(ml_dtypes.bfloat16).astype(np.float64), axis, -1)
    blocks = v.reshape(v.shape[:-1] + (-1, 32))
    amax = np.abs(blocks).max(-1, keepdims=True)
    byte = np.maximum(np.where(amax > 0, np.frexp(amax)[1] - 1 + 127, 0) - down, 1)
    scale = np.exp2(byte - 127.0)
    codes = (blocks / scale).astype(np.float32).astype(dtype).astype(np.float64)
    return np.moveaxis((codes * scale).reshape(v.shape), -1, axis)


WIDE = False


def mx_kscale(k):
    if not WIDE:
        return np.ones(k)
    levels = np.array([10, -10, 5, -5, 0])
    if k % 512:
        return np.exp2(np.random.permutation(np.resize(levels, k // 32))).repeat(32)
    a = np.empty((k // 512, 16))
    for p in range(k // 512):
        a[p, :8] = np.random.permutation(np.resize(levels, 8))
        for g in range(8):
            far = levels[np.abs(levels - a[p, g]) >= 10]
            a[p, g + 8] = far[np.random.randint(len(far))]
    return np.exp2(a.ravel()).repeat(32)


BF16 = ml_dtypes.bfloat16


def bf(x):
    return np.asarray(x, np.float32).astype(BF16)


def f64(x):
    return np.asarray(x).astype(np.float64)

def planes(Y):
    n, m = Y.shape
    b = f64(bf(Y)).reshape(n // 32, 32, m)
    amax = np.abs(b).max(1)
    byte = np.clip(np.where(amax > 0, np.frexp(amax)[1] - 1 + 127 - 7, 1), 1, 254)
    codes = (b * np.exp2(127.0 - byte)[:, None, :]).reshape(n, m).astype(np.float32).astype(ml_dtypes.float8_e4m3fn).view(np.uint8)
    words = codes.reshape(n // 512, 128, 4, m).transpose(0, 1, 3, 2)
    return np.ascontiguousarray(words), np.ascontiguousarray(byte.astype(np.uint8).reshape(n // 512, 16, m))


B, S, E, H = 4, 384, 1024, 2048
KEEP = 0.8

def setup_inputs():
    s = mx_kscale(E)
    spread = np.exp(0.8 * np.random.randn(H))
    token_rows = np.random.randn(B, S, E) * s
    expand = np.random.randn(E, H) / np.sqrt(E) * spread / s[:, None]
    bias = 0.5 * np.random.randn(H) * spread
    pos = 0.5 * np.random.randn(H, S) * spread[:, None]
    mask = (np.random.rand(H, B, S) < KEEP) / KEEP
    return {"token_rows": bf(token_rows), "expand": bf(expand), "bias": bf(bias),
            "pos": bf(pos), "mask": bf(mask)}

def reference(token_rows, expand, bias, pos, mask):
    x = mxq(f64(token_rows).reshape(B * S, E), 1, "e4m3")
    w = mxq(f64(expand), 0, "e4m3")
    wide = w.T @ x.T
    y = (wide.reshape(H, B, S) + f64(bias)[:, None, None] + f64(pos)[:, None, :]) * f64(mask)
    Y = y.reshape(H, B * S)
    words, scales = planes(Y)
    return y, words, scales

@@ -1,0 +1,303 @@
+from contextlib import ExitStack
+
+import concourse.mybir as mybir
+from concourse.masks import make_identity
+
+B, S, E, H = 4, 384, 1024, 2048
+M = B * S
+FLOPS = 2 * M * E * H
+
+F32 = mybir.dt.float32
+BF16 = mybir.dt.bfloat16
+I32 = mybir.dt.int32
+U32 = mybir.dt.uint32
+U8 = mybir.dt.uint8
+FP8X4 = mybir.dt.float8_e4m3fn_x4
+ADD = mybir.AluOpType.add
+MULT = mybir.AluOpType.mult
+
+P = 128
+PACK = 4
+KP = P * PACK
+PASSES = E // KP
+GROUPS = H // KP
+NC = 512
+CHUNKS = M // NC
+UNITS = GROUPS * CHUNKS
+ORDER = [(g, n) for n in range(CHUNKS) for g in (0, 1)] + [(g, n) for g in (2, 3) for n in range(CHUNKS)]
+SHARE = 192
+HELD = 64
+PIECES = [(u, 0, NC, SHARE) for u in range(UNITS - 2)] + [(10, 0, NC, 64), (11, 0, 256, 64), (11, 256, 512, 0)]
+QUANTIZE_AT = {k: [k - 2] for k in range(2, 13)}
+GROUP_W_AT = {3: (2, 0), 4: (2, 1), 6: (3, 0), 7: (3, 1)}
+
+
+def tile_factorized_embedding_width_rows_g2_kernel(
+    tc, token_rows, expand, bias, pos, mask, out_0, out_1, out_2
+):
+    nc = tc.nc
+    tokens = token_rows.rearrange("b s e -> (b s) e")
+    mask_rows = mask.rearrange("h b s -> h (b s)")
+    y_rows = out_0.rearrange("h b s -> h (b s)")
+    words_out = out_1.rearrange("g p m t -> g p (m t)").bitcast(I32)
+    scales_out = out_2.bitcast(I32)
+
+    with ExitStack() as ctx:
+        keep = ctx.enter_context(tc.tile_pool(name="keep", bufs=1))
+        ring = ctx.enter_context(tc.tile_pool(name="ring", bufs=3))
+        psum = ctx.enter_context(tc.psum_pool(name="psum", bufs=1))
+        ctx.enter_context(tc.manual_schedule())
+
+        ident = keep.tile([P, P], F32, name="ident")
+        bias_sb = keep.tile([P, GROUPS, 16], BF16, name="bias_sb")
+        x_codes = keep.tile([P, PASSES, M], U32, name="x_codes", align_bytes=64)
+        x_scales = keep.tile([P, PASSES, M], U8, name="x_scales", align_bytes=64)
+        y_scales = keep.tile([P, M], U8, name="y_scales", align_bytes=64)
+        x_raw = {}
+
+        w_raw, w_grouped, w_codes, w_scales = {}, {}, {}, {}
+        x_grouped, pos_sb, mask_sb, y_sb, y_words, y_grouped, acc = {}, {}, {}, {}, {}, {}, {}
+
+        def rows(g):
+            return slice(KP * g, KP * (g + 1))
+
+        def cols(n, lo=0, hi=NC):
+            return slice(NC * n + lo, NC * n + hi)
+
+        def load_w(g, c):
+            if c == 0:
+                w_raw[g] = ring.tile([P, PASSES, PACK, KP], BF16, name="w_raw", tag="w_raw", bufs=2)
+            nc.sync.dma_start(out=w_raw[g][:, c], in_=expand[rows(c), rows(g)].rearrange("(p j) h -> p j h", j=PACK))
+
+        def load_x(n, a0, a1):
+            if a0 == 0:
+                x_raw[n] = ring.tile([P, NC // P, E], BF16, name="x_raw", tag="big", bufs=9)
+            nc.sync.dma_start(
+                out=x_raw[n][:, a0:a1, :],
+                in_=tokens[NC * n + P * a0 : NC * n + P * a1, :].rearrange("(a p) e -> p a e", p=P),
+            )
+
+        def load_pos(g):
+            pos_sb[g] = ring.tile([P, PACK, 2 * S], BF16, name="pos_sb", tag="pos_sb")
+            nc.sync.dma_start(out=pos_sb[g][:, :, 0:S], in_=pos[rows(g), :].rearrange("(p t) s -> p t s", t=PACK))
+
+        def repeat_pos(g):
+            nc.scalar.copy(out=pos_sb[g][:, :, S : 2 * S], in_=pos_sb[g][:, :, 0:S])
+
+        def load_mask(g, n0, n1):
+            part = ring.tile([P, PACK, NC * (n1 - n0)], BF16, name="mask_sb", tag="mask_%d" % (n1 - n0), bufs=2)
+            nc.sync.dma_start(
+                out=part[:], in_=mask_rows[rows(g), NC * n0 : NC * n1].rearrange("(p t) m -> p t m", t=PACK)
+            )
+            for n in range(n0, n1):
+                mask_sb[ORDER.index((g, n))] = part[:, :, cols(n - n0)]
+
+        def group_w(g, c, copy, a0=0, a1=KP // 8):
+            if (g, c) not in w_grouped:
+                w_grouped[g, c] = ring.tile([P, PACK * KP], BF16, name="w_grouped", tag="w_grouped", align_bytes=64)
+            dst = w_grouped[g, c][:].rearrange("p (t a e j) -> p a t e j", t=PACK, e=2, j=PACK)
+            src = w_raw[g][:, c].rearrange("p j (a e t) -> p a t e j", e=2, t=PACK)
+            copy(out=dst[:, a0:a1], in_=src[:, a0:a1])
+
+        def quantize_w(g, c):
+            if c == 0:
+                w_codes[g] = ring.tile([P, PASSES, KP], U32, name="w_codes", tag="w_codes", bufs=2, align_bytes=64)
+                w_scales[g] = ring.tile([P, PASSES, KP], U8, name="w_scales", tag="w_scales", bufs=2, align_bytes=64)
+            nc.vector.quantize_mx(
+                out=w_codes[g][:, c, :].bitcast(FP8X4), scales=w_scales[g][:, c, :], in_=w_grouped[g, c][:]
+            )
+
+        def turn_x(n, c, h, bank_no):
+            if h == 0:
+                x_grouped[n, c] = ring.tile([P, PACK * NC], BF16, name="x_grouped", tag="x_grouped", align_bytes=64)
+            bank = psum.tile([P, 2, 2, P], F32, name="turned", tag="bank%d" % bank_no)
+            for a in range(2):
+                words = x_raw[n][:, 2 * h + a, :].bitcast(F32)
+                for u in range(2):
+                    nc.tensor.transpose(bank[:, a, u, :], words[:, 256 * c + u : 256 * (c + 1) : 2], ident[:])
+            dst = x_grouped[n, c][:].bitcast(F32)[:, 512 * h : 512 * (h + 1)]
+            nc.scalar.copy(
+                out=dst.rearrange("p (a r u) -> p a r u", a=2, u=2), in_=bank[:].rearrange("p a u r -> p a r u")
+            )
+
+        def quantize_x(n, c, lo=0, hi=NC):
+            nc.vector.quantize_mx(
+                out=x_codes[:, c, cols(n, lo, hi)].bitcast(FP8X4),
+                scales=x_scales[:, c, cols(n, lo, hi)],
+                in_=x_grouped[n, c][:, PACK * lo : PACK * hi],
+            )
+
+        def multiply(u, order=[(t, c) for t in range(PACK) for c in range(PASSES)]):
+            g, n = ORDER[u]
+            for t, c in order:
+                if c == 0:
+                    acc[u, t] = psum.tile([P, NC], F32, name="acc", tag="bank%d" % (PACK * (u % 2) + t))
+                nc.tensor.matmul_mx(
+                    out=acc[u, t][:],
+                    lhsT=w_codes[g][:, c, P * t : P * (t + 1)].bitcast(FP8X4),
+                    lhsT_scale=w_scales[g][:, c, P * t : P * (t + 1)],
+                    rhs=x_codes[:, c, cols(n)].bitcast(FP8X4),
+                    rhs_scale=x_scales[:, c, cols(n)],
+                    start=(c == 0),
+                    stop=(c == PASSES - 1),
+                )
+
+        def add_terms(k, t, a, b):
+            u, lo, hi, share = PIECES[k]
+            g, n = ORDER[u]
+            if k not in y_sb:
+                y_sb[k] = ring.tile([P, PACK, hi - lo], F32, name="y_sb", tag="big", bufs=9)
+            first = (NC * n) % S + lo
+            nc.vector.scalar_tensor_tensor(
+                out=y_sb[k][:, t, a:b],
+                in0=acc[u, t][:, lo + a : lo + b],
+                scalar=bias_sb[:, g, t : t + 1],
+                in1=pos_sb[g][:, t, first + a : first + b],
+                op0=ADD,
+                op1=ADD,
+            )
+
+        def apply_mask(engine, k, t0, t1, a, b):
+            u, lo, hi, share = PIECES[k]
+            part = y_sb[k][:, t0:t1, a:b]
+            engine.tensor_tensor(out=part, in0=part, in1=mask_sb[u][:, t0:t1, lo + a : lo + b], op=MULT)
+
+        def group_y(k, on_vector=False):
+            u, lo, hi, share = PIECES[k]
+            y_grouped[k] = ring.tile(
+                [P, PACK * (hi - lo)], BF16, name="y_grouped", tag="y_grouped", bufs=4, align_bytes=64
+            )
+            dst = y_grouped[k][:].rearrange("p (c i t) -> p c t i", i=4, t=PACK)
+            src = y_sb[k][:].rearrange("p t (c i) -> p c t i", i=4)
+            if on_vector:
+                nc.vector.tensor_copy(out=dst, in_=src)
+            else:
+                nc.scalar.copy(out=dst, in_=src)
+
+        def quantize_y(k):
+            u, lo, hi, share = PIECES[k]
+            g, n = ORDER[u]
+            y_words[k] = ring.tile([P, hi - lo], U32, name="y_words", tag="y_words", bufs=6, align_bytes=64)
+            nc.vector.quantize_mx(
+                out=y_words[k][:].bitcast(FP8X4),
+                scales=y_scales[PACK * g : P, cols(n, lo, hi)],
+                in_=y_grouped[k][:],
+            )
+
+        def store_y(k):
+            u, lo, hi, share = PIECES[k]
+            g, n = ORDER[u]
+            nc.sync.dma_start(
+                out=y_rows[rows(g), cols(n, lo, hi)].rearrange("(p t) m -> p t m", t=PACK), in_=y_sb[k][:]
+            )
+
+        def store_words(k):
+            u, lo, hi, share = PIECES[k]
+            g, n = ORDER[u]
+            nc.sync.dma_start(out=words_out[g, :, cols(n, lo, hi)], in_=y_words[k][:].bitcast(I32))
+
+        def store_scales(q):
+            nc.scalar.dma_start(
+                out=scales_out[:, 4 * q : 4 * q + 4, :], in_=y_scales[32 * q : 32 * q + 16, :].bitcast(I32)
+            )
+
+        nc.scalar.dma_start(out=bias_sb[:, :, 0:PACK], in_=bias.rearrange("(g p t) -> p g t", g=GROUPS, t=PACK))
+        make_identity(nc, ident[:])
+        load_x(0, 0, 2)
+        load_w(0, 0)
+        load_x(0, 2, 4)
+        load_w(0, 1)
+        load_pos(0)
+        load_w(1, 0)
+        load_w(1, 1)
+        load_mask(0, 0, 1)
+        load_pos(1)
+        load_x(1, 0, 2)
+        load_x(1, 2, 4)
+        load_mask(1, 0, 1)
+        load_mask(0, 1, 3)
+        load_x(2, 0, 4)
+        load_mask(1, 1, 3)
+
+        turn_x(0, 0, 0, 4)
+        turn_x(0, 1, 0, 5)
+        group_w(0, 0, nc.vector.tensor_copy)
+        quantize_x(0, 0, 0, 256)
+        quantize_w(0, 0)
+        quantize_x(0, 1, 0, 256)
+        turn_x(0, 0, 1, 6)
+        turn_x(0, 1, 1, 7)
+        group_w(0, 1, nc.vector.tensor_copy)
+        repeat_pos(0)
+        quantize_x(0, 0, 256, 512)
+        quantize_w(0, 1)
+        quantize_x(0, 1, 256, 512)
+        multiply(0)
+        group_w(1, 0, nc.scalar.copy)
+        group_w(1, 1, nc.scalar.copy)
+        repeat_pos(1)
+        load_w(2, 0)
+        load_w(2, 1)
+        load_pos(2)
+        load_mask(2, 0, 3)
+        load_w(3, 0)
+        load_w(3, 1)
+        load_mask(3, 0, 3)
+
+        last = len(PIECES) - 1
+        for k in range(last + 1):
+            u, lo, hi, share = PIECES[k]
+            width = hi - lo
+            if k > 0 and PIECES[k - 1][3]:
+                before = PIECES[k - 1][2] - PIECES[k - 1][1]
+                add_terms(k - 1, PACK - 1, before - HELD, before)
+                apply_mask(nc.gpsimd, k - 1, 0, PACK, before - PIECES[k - 1][3], before)
+            for t in range(PACK - 1):
+                add_terms(k, t, 0, width)
+            add_terms(k, PACK - 1, 0, width - HELD if share else width)
+
+            if k in (1, 3):
+                turn_x(k // 2 + 1, 0, 1, 2)
+                turn_x(k // 2 + 1, 1, 1, 0)
+            if k >= 1:
+                group_y(k - 1)
+            if k in (0, 2):
+                turn_x(k // 2 + 1, 0, 0, 0)
+                turn_x(k // 2 + 1, 1, 0, 1)
+            if k in GROUP_W_AT:
+                group_w(*GROUP_W_AT[k], nc.scalar.copy)
+            if k in (4, 7):
+                repeat_pos(k // 3 + 1)
+
+            for j in QUANTIZE_AT.get(k, []):
+                quantize_y(j)
+            if k == 0:
+                quantize_w(1, 0)
+            if k - 1 in GROUP_W_AT:
+                quantize_w(*GROUP_W_AT[k - 1])
+            if k in (1, 3):
+                quantize_x(k // 2 + 1, 0)
+            apply_mask(nc.vector, k, 2, PACK, 0, width - share)
+            if k == 0:
+                quantize_w(1, 1)
+            if k in (1, 3):
+                quantize_x(k // 2 + 1, 1)
+            if lo == 0 and u + 1 < UNITS:
+                multiply(u + 1)
+            apply_mask(nc.vector, k, 0, 2, 0, width - share)
+
+            if k >= 1:
+                store_y(k - 1)
+            for j in QUANTIZE_AT.get(k, []):
+                store_words(j)
+            if k == 5:
+                load_pos(3)
+
+        store_y(last)
+        quantize_y(last - 1)
+        group_y(last, on_vector=True)
+        store_words(last - 1)
+        quantize_y(last)
+        store_words(last)
+        for q in range(4):
+            store_scales(q)

@@ -23,12 +23,30 @@ PASSES = E // KP
 GROUPS = H // KP
 NC = 512
 CHUNKS = M // NC
-UNITS = GROUPS * CHUNKS
-ORDER = [(g, n) for n in range(CHUNKS) for g in (0, 1)] + [(g, n) for g in (2, 3) for n in range(CHUNKS)]
-SHARE = 192
+HALF = NC // 2
+W_SPLIT = 2
 HELD = 64
-PIECES = [(u, 0, NC, SHARE) for u in range(UNITS - 2)] + [(10, 0, NC, 64), (11, 0, 256, 64), (11, 256, 512, 0)]
-QUANTIZE_AT = {k: [k - 2] for k in range(2, 13)}
+SHARE = 192
+TAIL_SHARE = 64
+
+BY_CHUNK = [[(t, n) for t in range(PACK)] for n in range(CHUNKS)]
+BY_ROW = [[divmod(PACK * s + j, CHUNKS) for j in range(PACK)] for s in range(CHUNKS)]
+UNITS = (
+    [(g, BY_CHUNK[n]) for n in range(CHUNKS) for g in (0, 1)]
+    + [(2, banks) for banks in BY_CHUNK]
+    + [(3, banks) for banks in BY_CHUNK]
+)
+STEPS = [(u, 0, NC, SHARE) for u in range(10)] + [(10, 0, NC, TAIL_SHARE), (11, 0, HALF, TAIL_SHARE), (11, HALF, NC, 0)]
+BLOCKS = (
+    [(g, n, 0, NC) for n in range(CHUNKS) for g in (0, 1)]
+    + [(2, n, 0, NC) for n in range(CHUNKS)]
+    + [(3, 0, 0, NC), (3, 1, 0, NC), (3, 2, 0, HALF), (3, 2, HALF, NC)]
+)
+Y_REGIONS = {0: [(0, 512), (512, 1536)], 1: [(0, 512), (512, 1536)], 2: [(0, 512), (512, 1024), (1024, 1536)], 3: [(0, 512), (512, 1024), (1024, 1280), (1280, 1536)]}
+MASK_REGIONS = {0: [(0, 512), (512, 1536)], 1: [(0, 512), (512, 1536)], 2: [(0, 1536)], 3: [(0, 1536)]}
+Y_STORE_AFTER = {0: (0, 0), 1: (1, 0), 4: (0, 1), 5: (1, 1), 6: (2, 0), 7: (2, 1), 8: (2, 2), 9: (3, 0), 10: (3, 1), 11: (3, 2), 12: (3, 3)}
+GROUP_Y_AT = {1: [0], 2: [1], 3: [2], 4: [3], 5: [4], 6: [5], 7: [6], 8: [7], 9: [8], 10: [9], 11: [10], 12: [11]}
+QUANTIZE_AT = {2: [0], 3: [1], 4: [2], 5: [3], 6: [4], 7: [5], 8: [6], 9: [7], 10: [8], 11: [9], 12: [10]}
 GROUP_W_AT = {3: (2, 0), 4: (2, 1), 6: (3, 0), 7: (3, 1)}
 
 
@@ -53,7 +71,7 @@ def tile_factorized_embedding_width_rows_g2_kernel(
         x_codes = keep.tile([P, PASSES, M], U32, name="x_codes", align_bytes=64)
         x_scales = keep.tile([P, PASSES, M], U8, name="x_scales", align_bytes=64)
         y_scales = keep.tile([P, M], U8, name="y_scales", align_bytes=64)
-        x_raw = {}
+        x_raw = ring.tile([P, M // P, E], BF16, name="x_raw", tag="big")
 
         w_raw, w_grouped, w_codes, w_scales = {}, {}, {}, {}
         x_grouped, pos_sb, mask_sb, y_sb, y_words, y_grouped, acc = {}, {}, {}, {}, {}, {}, {}
@@ -64,40 +82,53 @@ def tile_factorized_embedding_width_rows_g2_kernel(
         def cols(n, lo=0, hi=NC):
             return slice(NC * n + lo, NC * n + hi)
 
-        def load_w(g, c):
-            if c == 0:
-                w_raw[g] = ring.tile([P, PASSES, PACK, KP], BF16, name="w_raw", tag="w_raw", bufs=2)
-            nc.sync.dma_start(out=w_raw[g][:, c], in_=expand[rows(c), rows(g)].rearrange("(p j) h -> p j h", j=PACK))
+        def load_first_w(g, c):
+            if (g, c) == (0, 0):
+                w_raw["first"] = keep.tile([P, 2, PASSES, PACK, KP], BF16, name="w_first", tag="w_raw")
+            w_raw[g, c] = w_raw["first"][:, g, c]
+            nc.sync.dma_start(out=w_raw[g, c], in_=expand[rows(c), rows(g)].rearrange("(p j) h -> p j h", j=PACK))
 
-        def load_x(n, a0, a1):
-            if a0 == 0:
-                x_raw[n] = ring.tile([P, NC // P, E], BF16, name="x_raw", tag="big", bufs=9)
+        def load_last_w():
+            both = keep.tile([P, PASSES, PACK, 2 * KP], BF16, name="w_last", tag="w_raw")
+            for c in range(PASSES):
+                nc.sync.dma_start(
+                    out=both[:, c], in_=expand[rows(c), 2 * KP : 4 * KP].rearrange("(p j) h -> p j h", j=PACK)
+                )
+                for g in (2, 3):
+                    w_raw[g, c] = both[:, c, :, rows(g - 2)]
+
+        def load_x(h0, h1):
             nc.sync.dma_start(
-                out=x_raw[n][:, a0:a1, :],
-                in_=tokens[NC * n + P * a0 : NC * n + P * a1, :].rearrange("(a p) e -> p a e", p=P),
+                out=x_raw[:, 2 * h0 : 2 * h1, :].rearrange("p (h a) e -> p h (a e)", a=2),
+                in_=tokens[HALF * h0 : HALF * h1, :].rearrange("(h p a) e -> p h (a e)", p=P, a=2),
             )
 
         def load_pos(g):
-            pos_sb[g] = ring.tile([P, PACK, 2 * S], BF16, name="pos_sb", tag="pos_sb")
+            pos_sb[g] = ring.tile([P, PACK, 2 * S], BF16, name="pos_sb", tag="pos_sb", bufs=4)
             nc.sync.dma_start(out=pos_sb[g][:, :, 0:S], in_=pos[rows(g), :].rearrange("(p t) s -> p t s", t=PACK))
 
         def repeat_pos(g):
             nc.scalar.copy(out=pos_sb[g][:, :, S : 2 * S], in_=pos_sb[g][:, :, 0:S])
 
-        def load_mask(g, n0, n1):
-            part = ring.tile([P, PACK, NC * (n1 - n0)], BF16, name="mask_sb", tag="mask_%d" % (n1 - n0), bufs=2)
-            nc.sync.dma_start(
-                out=part[:], in_=mask_rows[rows(g), NC * n0 : NC * n1].rearrange("(p t) m -> p t m", t=PACK)
-            )
-            for n in range(n0, n1):
-                mask_sb[ORDER.index((g, n))] = part[:, :, cols(n - n0)]
+        def window(tile, regions, m0, m1):
+            r0, r1 = [r for r in regions if r[0] <= m0 < r[1]][0]
+            return tile[:, PACK * r0 : PACK * r1].rearrange("p (t m) -> p t m", t=PACK)[:, :, m0 - r0 : m1 - r0]
 
-        def group_w(g, c, copy, a0=0, a1=KP // 8):
+        def load_mask(g, r=0):
+            if r == 0:
+                mask_sb[g] = ring.tile([P, PACK * M], BF16, name="mask_sb", tag="mask_sb", bufs=4)
+            m0, m1 = MASK_REGIONS[g][r]
+            nc.sync.dma_start(
+                out=window(mask_sb[g], MASK_REGIONS[g], m0, m1),
+                in_=mask_rows[rows(g), m0:m1].rearrange("(p t) m -> p t m", t=PACK),
+            )
+
+        def group_w(g, c, copy, t0=0, t1=PACK):
             if (g, c) not in w_grouped:
-                w_grouped[g, c] = ring.tile([P, PACK * KP], BF16, name="w_grouped", tag="w_grouped", align_bytes=64)
+                w_grouped[g, c] = ring.tile([P, PACK * KP], BF16, name="w_grouped", tag="w_grouped", bufs=2, align_bytes=64)
             dst = w_grouped[g, c][:].rearrange("p (t a e j) -> p a t e j", t=PACK, e=2, j=PACK)
-            src = w_raw[g][:, c].rearrange("p j (a e t) -> p a t e j", e=2, t=PACK)
-            copy(out=dst[:, a0:a1], in_=src[:, a0:a1])
+            src = w_raw[g, c].rearrange("p j (a e t) -> p a t e j", e=2, t=PACK)
+            copy(out=dst[:, :, t0:t1], in_=src[:, :, t0:t1])
 
         def quantize_w(g, c):
             if c == 0:
@@ -109,16 +140,21 @@ def tile_factorized_embedding_width_rows_g2_kernel(
 
         def turn_x(n, c, h, bank_no):
             if h == 0:
-                x_grouped[n, c] = ring.tile([P, PACK * NC], BF16, name="x_grouped", tag="x_grouped", align_bytes=64)
+                x_grouped[n, c] = ring.tile([P, PACK * NC], BF16, name="x_grouped", tag="x_grouped", bufs=2, align_bytes=64)
             bank = psum.tile([P, 2, 2, P], F32, name="turned", tag="bank%d" % bank_no)
             for a in range(2):
-                words = x_raw[n][:, 2 * h + a, :].bitcast(F32)
+                words = x_raw[:, 4 * n + 2 * h + a, :].bitcast(F32)
                 for u in range(2):
                     nc.tensor.transpose(bank[:, a, u, :], words[:, 256 * c + u : 256 * (c + 1) : 2], ident[:])
             dst = x_grouped[n, c][:].bitcast(F32)[:, 512 * h : 512 * (h + 1)]
             nc.scalar.copy(
-                out=dst.rearrange("p (a r u) -> p a r u", a=2, u=2), in_=bank[:].rearrange("p a u r -> p a r u")
+                out=dst.rearrange("p (r a u) -> p r a u", a=2, u=2), in_=bank[:].rearrange("p a u r -> p r a u")
             )
+
+        def turn_chunk(n):
+            for h in range(2):
+                for c in range(PASSES):
+                    turn_x(n, c, h, (2 * h + c) % 3)
 
         def quantize_x(n, c, lo=0, hi=NC):
             nc.vector.quantize_mx(
@@ -127,177 +163,214 @@ def tile_factorized_embedding_width_rows_g2_kernel(
                 in_=x_grouped[n, c][:, PACK * lo : PACK * hi],
             )
 
-        def multiply(u, order=[(t, c) for t in range(PACK) for c in range(PASSES)]):
-            g, n = ORDER[u]
-            for t, c in order:
-                if c == 0:
-                    acc[u, t] = psum.tile([P, NC], F32, name="acc", tag="bank%d" % (PACK * (u % 2) + t))
-                nc.tensor.matmul_mx(
-                    out=acc[u, t][:],
-                    lhsT=w_codes[g][:, c, P * t : P * (t + 1)].bitcast(FP8X4),
-                    lhsT_scale=w_scales[g][:, c, P * t : P * (t + 1)],
-                    rhs=x_codes[:, c, cols(n)].bitcast(FP8X4),
-                    rhs_scale=x_scales[:, c, cols(n)],
-                    start=(c == 0),
-                    stop=(c == PASSES - 1),
-                )
+        def multiply(u):
+            g, banks = UNITS[u]
+            for j, (t, n) in enumerate(banks):
+                acc[u, j] = psum.tile([P, NC], F32, name="acc", tag="bank%d" % (PACK * (u % 2) + j))
+                for c in range(PASSES):
+                    nc.tensor.matmul_mx(
+                        out=acc[u, j][:],
+                        lhsT=w_codes[g][:, c, P * t : P * (t + 1)].bitcast(FP8X4),
+                        lhsT_scale=w_scales[g][:, c, P * t : P * (t + 1)],
+                        rhs=x_codes[:, c, cols(n)].bitcast(FP8X4),
+                        rhs_scale=x_scales[:, c, cols(n)],
+                        start=(c == 0),
+                        stop=(c == PASSES - 1),
+                    )
 
-        def add_terms(k, t, a, b):
-            u, lo, hi, share = PIECES[k]
-            g, n = ORDER[u]
-            if k not in y_sb:
-                y_sb[k] = ring.tile([P, PACK, hi - lo], F32, name="y_sb", tag="big", bufs=9)
+        def block_of_y(g, n, lo, hi):
+            return window(y_sb[g], Y_REGIONS[g], NC * n + lo, NC * n + hi)
+
+        def step_views(k):
+            u, lo, hi, share = STEPS[k]
+            g, banks = UNITS[u]
+            if g == 7:
+                s = u - 6
+                flat = slice(PACK * NC * s, PACK * NC * (s + 1))
+                y_part = y_sb[g][:, flat].rearrange("p (j m) -> p j m", j=PACK)
+                mask_part = mask_sb[g][:, flat].rearrange("p (j m) -> p j m", j=PACK)
+                return y_part, mask_part
+            n = banks[0][1]
+            return block_of_y(g, n, lo, hi), window(mask_sb[g], MASK_REGIONS[g], NC * n + lo, NC * n + hi)
+
+        def add_terms(k, j, a, b):
+            u, lo, hi, share = STEPS[k]
+            g, banks = UNITS[u]
+            if g not in y_sb:
+                y_sb[g] = ring.tile([P, PACK * M], F32, name="y_sb", tag="big")
+            y_part, mask_part = step_views(k)
+            t, n = banks[j]
             first = (NC * n) % S + lo
             nc.vector.scalar_tensor_tensor(
-                out=y_sb[k][:, t, a:b],
-                in0=acc[u, t][:, lo + a : lo + b],
+                out=y_part[:, j, a:b],
+                in0=acc[u, j][:, lo + a : lo + b],
                 scalar=bias_sb[:, g, t : t + 1],
                 in1=pos_sb[g][:, t, first + a : first + b],
                 op0=ADD,
                 op1=ADD,
             )
 
-        def apply_mask(engine, k, t0, t1, a, b):
-            u, lo, hi, share = PIECES[k]
-            part = y_sb[k][:, t0:t1, a:b]
-            engine.tensor_tensor(out=part, in0=part, in1=mask_sb[u][:, t0:t1, lo + a : lo + b], op=MULT)
-
-        def group_y(k, on_vector=False):
-            u, lo, hi, share = PIECES[k]
-            y_grouped[k] = ring.tile(
-                [P, PACK * (hi - lo)], BF16, name="y_grouped", tag="y_grouped", bufs=4, align_bytes=64
+        def apply_mask(engine, k, j0, j1, a, b):
+            y_part, mask_part = step_views(k)
+            engine.tensor_tensor(
+                out=y_part[:, j0:j1, a:b], in0=y_part[:, j0:j1, a:b], in1=mask_part[:, j0:j1, a:b], op=MULT
             )
-            dst = y_grouped[k][:].rearrange("p (c i t) -> p c t i", i=4, t=PACK)
-            src = y_sb[k][:].rearrange("p t (c i) -> p c t i", i=4)
-            if on_vector:
-                nc.vector.tensor_copy(out=dst, in_=src)
-            else:
-                nc.scalar.copy(out=dst, in_=src)
 
-        def quantize_y(k):
-            u, lo, hi, share = PIECES[k]
-            g, n = ORDER[u]
-            y_words[k] = ring.tile([P, hi - lo], U32, name="y_words", tag="y_words", bufs=6, align_bytes=64)
+        def group_y(i, copy):
+            g, n, lo, hi = BLOCKS[i]
+            y_grouped[i] = ring.tile(
+                [P, PACK * (hi - lo)], BF16, name="y_grouped", tag="y_grouped", bufs=3, align_bytes=64
+            )
+            copy(
+                out=y_grouped[i][:].rearrange("p (c i t) -> p c t i", i=4, t=PACK),
+                in_=block_of_y(g, n, lo, hi).rearrange("p t (c i) -> p c t i", i=4),
+            )
+
+        def quantize_y(i):
+            g, n, lo, hi = BLOCKS[i]
+            if g not in y_words:
+                y_words[g] = ring.tile([P, M], U32, name="y_words", tag="y_words", bufs=2, align_bytes=64)
             nc.vector.quantize_mx(
-                out=y_words[k][:].bitcast(FP8X4),
+                out=y_words[g][:, cols(n, lo, hi)].bitcast(FP8X4),
                 scales=y_scales[PACK * g : P, cols(n, lo, hi)],
-                in_=y_grouped[k][:],
+                in_=y_grouped[i][:],
             )
 
-        def store_y(k):
-            u, lo, hi, share = PIECES[k]
-            g, n = ORDER[u]
+        def store_y_flat(g, f0, f1):
             nc.sync.dma_start(
-                out=y_rows[rows(g), cols(n, lo, hi)].rearrange("(p t) m -> p t m", t=PACK), in_=y_sb[k][:]
+                out=y_rows[rows(g), :].rearrange("(p t) m -> p (t m)", t=PACK)[:, f0:f1], in_=y_sb[g][:, f0:f1]
             )
 
-        def store_words(k):
-            u, lo, hi, share = PIECES[k]
-            g, n = ORDER[u]
-            nc.sync.dma_start(out=words_out[g, :, cols(n, lo, hi)], in_=y_words[k][:].bitcast(I32))
+        def store_y_region(g, r):
+            m0, m1 = Y_REGIONS[g][r]
+            nc.sync.dma_start(
+                out=y_rows[rows(g), m0:m1].rearrange("(p t) m -> p t m", t=PACK),
+                in_=window(y_sb[g], Y_REGIONS[g], m0, m1),
+            )
+
+        def store_after(k):
+            if k in Y_STORE_AFTER:
+                store_y_region(*Y_STORE_AFTER[k])
+
+        def store_words(g, m0, m1):
+            nc.sync.dma_start(out=words_out[g, :, m0:m1], in_=y_words[g][:, m0:m1].bitcast(I32))
 
         def store_scales(q):
             nc.scalar.dma_start(
                 out=scales_out[:, 4 * q : 4 * q + 4, :], in_=y_scales[32 * q : 32 * q + 16, :].bitcast(I32)
             )
 
-        nc.scalar.dma_start(out=bias_sb[:, :, 0:PACK], in_=bias.rearrange("(g p t) -> p g t", g=GROUPS, t=PACK))
         make_identity(nc, ident[:])
-        load_x(0, 0, 2)
-        load_w(0, 0)
-        load_x(0, 2, 4)
-        load_w(0, 1)
+        load_x(0, 1)
+        load_first_w(0, 0)
+        load_x(1, 2)
+        load_first_w(0, 1)
         load_pos(0)
-        load_w(1, 0)
-        load_w(1, 1)
-        load_mask(0, 0, 1)
+        nc.sync.dma_start(out=bias_sb[:, :, 0:PACK], in_=bias.rearrange("(g p t) -> p g t", g=GROUPS, t=PACK))
+        load_first_w(1, 0)
+        load_first_w(1, 1)
+        load_x(2, 3)
         load_pos(1)
-        load_x(1, 0, 2)
-        load_x(1, 2, 4)
-        load_mask(1, 0, 1)
-        load_mask(0, 1, 3)
-        load_x(2, 0, 4)
-        load_mask(1, 1, 3)
+        load_mask(0, 0)
+        load_x(3, 4)
+        load_mask(1, 0)
+        load_mask(0, 1)
+        load_x(4, 6)
+        load_mask(1, 1)
 
         turn_x(0, 0, 0, 4)
         turn_x(0, 1, 0, 5)
         group_w(0, 0, nc.vector.tensor_copy)
-        quantize_x(0, 0, 0, 256)
+        quantize_x(0, 0, 0, HALF)
         quantize_w(0, 0)
-        quantize_x(0, 1, 0, 256)
+        quantize_x(0, 1, 0, HALF)
         turn_x(0, 0, 1, 6)
         turn_x(0, 1, 1, 7)
         group_w(0, 1, nc.vector.tensor_copy)
         repeat_pos(0)
-        quantize_x(0, 0, 256, 512)
+        quantize_x(0, 0, HALF, NC)
         quantize_w(0, 1)
-        quantize_x(0, 1, 256, 512)
+        quantize_x(0, 1, HALF, NC)
         multiply(0)
         group_w(1, 0, nc.scalar.copy)
-        group_w(1, 1, nc.scalar.copy)
+        group_w(1, 1, nc.scalar.copy, 0, W_SPLIT)
         repeat_pos(1)
-        load_w(2, 0)
-        load_w(2, 1)
-        load_pos(2)
-        load_mask(2, 0, 3)
-        load_w(3, 0)
-        load_w(3, 1)
-        load_mask(3, 0, 3)
 
-        last = len(PIECES) - 1
+        last = len(STEPS) - 1
         for k in range(last + 1):
-            u, lo, hi, share = PIECES[k]
+            u, lo, hi, share = STEPS[k]
             width = hi - lo
-            if k > 0 and PIECES[k - 1][3]:
-                before = PIECES[k - 1][2] - PIECES[k - 1][1]
+            if k > 0 and STEPS[k - 1][3]:
+                before = STEPS[k - 1][2] - STEPS[k - 1][1]
                 add_terms(k - 1, PACK - 1, before - HELD, before)
-                apply_mask(nc.gpsimd, k - 1, 0, PACK, before - PIECES[k - 1][3], before)
-            for t in range(PACK - 1):
-                add_terms(k, t, 0, width)
+                apply_mask(nc.gpsimd, k - 1, 0, PACK, before - STEPS[k - 1][3], before)
+                store_after(k - 1)
+            for j in range(PACK - 1):
+                add_terms(k, j, 0, width)
             add_terms(k, PACK - 1, 0, width - HELD if share else width)
 
-            if k in (1, 3):
-                turn_x(k // 2 + 1, 0, 1, 2)
-                turn_x(k // 2 + 1, 1, 1, 0)
-            if k >= 1:
-                group_y(k - 1)
-            if k in (0, 2):
-                turn_x(k // 2 + 1, 0, 0, 0)
-                turn_x(k // 2 + 1, 1, 0, 1)
-            if k in GROUP_W_AT:
+            if k in (6, 7):
+                group_w(*GROUP_W_AT[k], nc.scalar.copy)
+            for i in GROUP_Y_AT.get(k, []):
+                group_y(i, nc.scalar.copy)
+            if k in (3, 4):
                 group_w(*GROUP_W_AT[k], nc.scalar.copy)
             if k in (4, 7):
                 repeat_pos(k // 3 + 1)
 
-            for j in QUANTIZE_AT.get(k, []):
-                quantize_y(j)
             if k == 0:
+                group_w(1, 1, nc.vector.tensor_copy, W_SPLIT)
                 quantize_w(1, 0)
-            if k - 1 in GROUP_W_AT:
-                quantize_w(*GROUP_W_AT[k - 1])
+                load_last_w()
+                load_pos(2)
+                load_mask(2)
+                load_pos(3)
+                load_mask(3)
             if k in (1, 3):
                 quantize_x(k // 2 + 1, 0)
-            apply_mask(nc.vector, k, 2, PACK, 0, width - share)
+                quantize_x(k // 2 + 1, 1)
+            if k in (5, 8):
+                quantize_w(*GROUP_W_AT[k - 1])
             if k == 0:
                 quantize_w(1, 1)
-            if k in (1, 3):
-                quantize_x(k // 2 + 1, 1)
-            if lo == 0 and u + 1 < UNITS:
+                turn_x(1, 0, 0, 0)
+                turn_x(1, 1, 0, 1)
+            if lo == 0 and u + 1 < len(UNITS):
                 multiply(u + 1)
-            apply_mask(nc.vector, k, 0, 2, 0, width - share)
+            if k == 0:
+                turn_x(1, 0, 1, 2)
+                turn_x(1, 1, 1, 0)
+            if k == 2:
+                turn_chunk(2)
+            if k in (3, 5, 8):
+                apply_mask(nc.vector, k, 0, PACK, 0, width - share)
+                quantize_y(k - 2)
+            elif k in (4, 7):
+                quantize_y(k - 2)
+                apply_mask(nc.vector, k, 0, PACK, 0, width - share)
+                quantize_w(*GROUP_W_AT[k - 1])
+            else:
+                if k >= 2:
+                    quantize_y(k - 2)
+                apply_mask(nc.vector, k, 2, PACK, 0, width - share)
+                apply_mask(nc.vector, k, 0, 2, 0, width - share)
+            if k == 6:
+                store_words(0, 0, M)
+            if k == 7:
+                store_words(1, 0, M)
+            if k == 9:
+                store_words(2, 0, 2 * NC)
+            if k == 10:
+                store_words(2, 2 * NC, M)
+            if k == 11:
+                store_words(3, 0, NC)
+            if k == 12:
+                store_words(3, NC, 2 * NC)
 
-            if k >= 1:
-                store_y(k - 1)
-            for j in QUANTIZE_AT.get(k, []):
-                store_words(j)
-            if k == 5:
-                load_pos(3)
-
-        store_y(last)
-        quantize_y(last - 1)
-        group_y(last, on_vector=True)
-        store_words(last - 1)
-        quantize_y(last)
-        store_words(last)
+        store_after(last)
+        quantize_y(11)
+        group_y(12, nc.vector.tensor_copy)
+        quantize_y(12)
+        store_words(3, 2 * NC, M)
         for q in range(4):
             store_scales(q)

@@ -26,8 +26,8 @@ CHUNKS = M // NC
 HALF = NC // 2
 W_SPLIT = 2
 HELD = 64
-SHARE = 192
-TAIL_SHARE = 64
+SHARE = 208
+TAIL_SHARE = 96
 
 BY_CHUNK = [[(t, n) for t in range(PACK)] for n in range(CHUNKS)]
 BY_ROW = [[divmod(PACK * s + j, CHUNKS) for j in range(PACK)] for s in range(CHUNKS)]
@@ -42,9 +42,9 @@ BLOCKS = (
     + [(2, n, 0, NC) for n in range(CHUNKS)]
     + [(3, 0, 0, NC), (3, 1, 0, NC), (3, 2, 0, HALF), (3, 2, HALF, NC)]
 )
-Y_REGIONS = {0: [(0, 512), (512, 1536)], 1: [(0, 512), (512, 1536)], 2: [(0, 512), (512, 1024), (1024, 1536)], 3: [(0, 512), (512, 1024), (1024, 1280), (1280, 1536)]}
-MASK_REGIONS = {0: [(0, 512), (512, 1536)], 1: [(0, 512), (512, 1536)], 2: [(0, 1536)], 3: [(0, 1536)]}
-Y_STORE_AFTER = {0: (0, 0), 1: (1, 0), 4: (0, 1), 5: (1, 1), 6: (2, 0), 7: (2, 1), 8: (2, 2), 9: (3, 0), 10: (3, 1), 11: (3, 2), 12: (3, 3)}
+Y_REGIONS = {0: [(0, 512), (512, 1536)], 1: [(0, 1536)], 2: [(0, 1024), (1024, 1536)], 3: [(0, 512), (512, 1024), (1024, 1536)]}
+MASK_REGIONS = {0: [(0, 512), (512, 1536)], 1: [(0, 1536)], 2: [(0, 1536)], 3: [(0, 1536)]}
+Y_STORE_AFTER = {0: (0, 0), 4: (0, 1), 5: (1, 0), 7: (2, 0), 8: (2, 1), 9: (3, 0), 10: (3, 1), 12: (3, 2)}
 GROUP_Y_AT = {1: [0], 2: [1], 3: [2], 4: [3], 5: [4], 6: [5], 7: [6], 8: [7], 9: [8], 10: [9], 11: [10], 12: [11]}
 QUANTIZE_AT = {2: [0], 3: [1], 4: [2], 5: [3], 6: [4], 7: [5], 8: [6], 9: [7], 10: [8], 11: [9], 12: [10]}
 GROUP_W_AT = {3: (2, 0), 4: (2, 1), 6: (3, 0), 7: (3, 1)}
@@ -67,7 +67,8 @@ def tile_factorized_embedding_width_rows_g2_kernel(
         ctx.enter_context(tc.manual_schedule())
 
         ident = keep.tile([P, P], F32, name="ident")
-        bias_sb = keep.tile([P, GROUPS, 16], BF16, name="bias_sb")
+        bias_rows = keep.tile([P, KP], BF16, name="bias_rows")
+        bias_sb = keep.tile([P, 2, GROUPS, 2], BF16, name="bias_sb")
         x_codes = keep.tile([P, PASSES, M], U32, name="x_codes", align_bytes=64)
         x_scales = keep.tile([P, PASSES, M], U8, name="x_scales", align_bytes=64)
         y_scales = keep.tile([P, M], U8, name="y_scales", align_bytes=64)
@@ -75,6 +76,9 @@ def tile_factorized_embedding_width_rows_g2_kernel(
 
         w_raw, w_grouped, w_codes, w_scales = {}, {}, {}, {}
         x_grouped, pos_sb, mask_sb, y_sb, y_words, y_grouped, acc = {}, {}, {}, {}, {}, {}, {}
+
+        def bias_of(g, t):
+            return bias_sb[:, t // 2, g, t % 2 : t % 2 + 1]
 
         def rows(g):
             return slice(KP * g, KP * (g + 1))
@@ -104,11 +108,8 @@ def tile_factorized_embedding_width_rows_g2_kernel(
             )
 
         def load_pos(g):
-            pos_sb[g] = ring.tile([P, PACK, 2 * S], BF16, name="pos_sb", tag="pos_sb", bufs=4)
-            nc.sync.dma_start(out=pos_sb[g][:, :, 0:S], in_=pos[rows(g), :].rearrange("(p t) s -> p t s", t=PACK))
-
-        def repeat_pos(g):
-            nc.scalar.copy(out=pos_sb[g][:, :, S : 2 * S], in_=pos_sb[g][:, :, 0:S])
+            pos_sb[g] = ring.tile([P, PACK, S], BF16, name="pos_sb", tag="pos_sb", bufs=4)
+            nc.sync.dma_start(out=pos_sb[g][:], in_=pos[rows(g), :].rearrange("(p t) s -> p t s", t=PACK))
 
         def window(tile, regions, m0, m1):
             r0, r1 = [r for r in regions if r[0] <= m0 < r[1]][0]
@@ -201,14 +202,17 @@ def tile_factorized_embedding_width_rows_g2_kernel(
             y_part, mask_part = step_views(k)
             t, n = banks[j]
             first = (NC * n) % S + lo
-            nc.vector.scalar_tensor_tensor(
-                out=y_part[:, j, a:b],
-                in0=acc[u, j][:, lo + a : lo + b],
-                scalar=bias_sb[:, g, t : t + 1],
-                in1=pos_sb[g][:, t, first + a : first + b],
-                op0=ADD,
-                op1=ADD,
-            )
+            wrap = S - first
+            for c0, c1 in ([(a, wrap), (wrap, b)] if a < wrap < b else [(a, b)]):
+                i0 = (first + c0) % S
+                nc.vector.scalar_tensor_tensor(
+                    out=y_part[:, j, c0:c1],
+                    in0=acc[u, j][:, lo + c0 : lo + c1],
+                    scalar=bias_of(g, t),
+                    in1=pos_sb[g][:, t, i0 : i0 + c1 - c0],
+                    op0=ADD,
+                    op1=ADD,
+                )
 
         def apply_mask(engine, k, j0, j1, a, b):
             y_part, mask_part = step_views(k)
@@ -229,7 +233,7 @@ def tile_factorized_embedding_width_rows_g2_kernel(
         def quantize_y(i):
             g, n, lo, hi = BLOCKS[i]
             if g not in y_words:
-                y_words[g] = ring.tile([P, M], U32, name="y_words", tag="y_words", bufs=2, align_bytes=64)
+                y_words[g] = ring.tile([P, M], U32, name="y_words", tag="y_words", bufs=3, align_bytes=64)
             nc.vector.quantize_mx(
                 out=y_words[g][:, cols(n, lo, hi)].bitcast(FP8X4),
                 scales=y_scales[PACK * g : P, cols(n, lo, hi)],
@@ -260,13 +264,14 @@ def tile_factorized_embedding_width_rows_g2_kernel(
                 out=scales_out[:, 4 * q : 4 * q + 4, :], in_=y_scales[32 * q : 32 * q + 16, :].bitcast(I32)
             )
 
+        nc.vector.memset(bias_rows[:], 0.0)
         make_identity(nc, ident[:])
         load_x(0, 1)
+        nc.sync.dma_start(out=bias_rows[0:GROUPS, :], in_=bias.rearrange("(g h) -> g h", g=GROUPS))
         load_first_w(0, 0)
         load_x(1, 2)
         load_first_w(0, 1)
         load_pos(0)
-        nc.sync.dma_start(out=bias_sb[:, :, 0:PACK], in_=bias.rearrange("(g p t) -> p g t", g=GROUPS, t=PACK))
         load_first_w(1, 0)
         load_first_w(1, 1)
         load_x(2, 3)
@@ -276,7 +281,6 @@ def tile_factorized_embedding_width_rows_g2_kernel(
         load_mask(1, 0)
         load_mask(0, 1)
         load_x(4, 6)
-        load_mask(1, 1)
 
         turn_x(0, 0, 0, 4)
         turn_x(0, 1, 0, 5)
@@ -286,15 +290,20 @@ def tile_factorized_embedding_width_rows_g2_kernel(
         quantize_x(0, 1, 0, HALF)
         turn_x(0, 0, 1, 6)
         turn_x(0, 1, 1, 7)
+        bias_bank = psum.tile([P, 2, P], F32, name="bias_bank", tag="bank0")
+        for u in range(2):
+            nc.tensor.transpose(bias_bank[:, u, :], bias_rows[:].bitcast(F32)[:, u : KP // 2 : 2], ident[:])
+        nc.scalar.copy(
+            out=bias_sb[:].rearrange("p u g e -> p (u g e)").bitcast(F32).rearrange("p (u g) -> p u g", u=2),
+            in_=bias_bank[:, :, 0:GROUPS],
+        )
         group_w(0, 1, nc.vector.tensor_copy)
-        repeat_pos(0)
         quantize_x(0, 0, HALF, NC)
         quantize_w(0, 1)
         quantize_x(0, 1, HALF, NC)
         multiply(0)
         group_w(1, 0, nc.scalar.copy)
         group_w(1, 1, nc.scalar.copy, 0, W_SPLIT)
-        repeat_pos(1)
 
         last = len(STEPS) - 1
         for k in range(last + 1):
@@ -315,8 +324,6 @@ def tile_factorized_embedding_width_rows_g2_kernel(
                 group_y(i, nc.scalar.copy)
             if k in (3, 4):
                 group_w(*GROUP_W_AT[k], nc.scalar.copy)
-            if k in (4, 7):
-                repeat_pos(k // 3 + 1)
 
             if k == 0:
                 group_w(1, 1, nc.vector.tensor_copy, W_SPLIT)

@@ -18,36 +18,39 @@ MULT = mybir.AluOpType.mult
 
 P = 128
 PACK = 4
-KP = P * PACK
-PASSES = E // KP
-GROUPS = H // KP
-NC = 512
-CHUNKS = M // NC
-HALF = NC // 2
-W_SPLIT = 2
-HELD = 64
-SHARE = 208
-TAIL_SHARE = 96
+SPAN = P * PACK
+PASSES = E // SPAN
+GROUPS = H // SPAN
+CHUNK = 512
+CHUNKS = M // CHUNK
+HALF = CHUNK // 2
+QUADRANT = 32
 
-BY_CHUNK = [[(t, n) for t in range(PACK)] for n in range(CHUNKS)]
-BY_ROW = [[divmod(PACK * s + j, CHUNKS) for j in range(PACK)] for s in range(CHUNKS)]
-UNITS = (
-    [(g, BY_CHUNK[n]) for n in range(CHUNKS) for g in (0, 1)]
-    + [(2, banks) for banks in BY_CHUNK]
-    + [(3, banks) for banks in BY_CHUNK]
+SHARE = 216
+SHORT_SHARE = 96
+HELD = 64
+
+UNITS = [(g, n) for n in range(CHUNKS) for g in (0, 1)] + [(g, n) for g in (2, 3) for n in range(CHUNKS)]
+STEPS = (
+    [(u, 0, CHUNK, SHARE) for u in range(len(UNITS) - 2)]
+    + [(len(UNITS) - 2, 0, CHUNK, SHORT_SHARE)]
+    + [(len(UNITS) - 1, 0, HALF, SHORT_SHARE), (len(UNITS) - 1, HALF, CHUNK, 0)]
 )
-STEPS = [(u, 0, NC, SHARE) for u in range(10)] + [(10, 0, NC, TAIL_SHARE), (11, 0, HALF, TAIL_SHARE), (11, HALF, NC, 0)]
-BLOCKS = (
-    [(g, n, 0, NC) for n in range(CHUNKS) for g in (0, 1)]
-    + [(2, n, 0, NC) for n in range(CHUNKS)]
-    + [(3, 0, 0, NC), (3, 1, 0, NC), (3, 2, 0, HALF), (3, 2, HALF, NC)]
-)
-Y_REGIONS = {0: [(0, 512), (512, 1536)], 1: [(0, 1536)], 2: [(0, 1024), (1024, 1536)], 3: [(0, 512), (512, 1024), (1024, 1536)]}
-MASK_REGIONS = {0: [(0, 512), (512, 1536)], 1: [(0, 1536)], 2: [(0, 1536)], 3: [(0, 1536)]}
-Y_STORE_AFTER = {0: (0, 0), 4: (0, 1), 5: (1, 0), 7: (2, 0), 8: (2, 1), 9: (3, 0), 10: (3, 1), 12: (3, 2)}
-GROUP_Y_AT = {1: [0], 2: [1], 3: [2], 4: [3], 5: [4], 6: [5], 7: [6], 8: [7], 9: [8], 10: [9], 11: [10], 12: [11]}
-QUANTIZE_AT = {2: [0], 3: [1], 4: [2], 5: [3], 6: [4], 7: [5], 8: [6], 9: [7], 10: [8], 11: [9], 12: [10]}
-GROUP_W_AT = {3: (2, 0), 4: (2, 1), 6: (3, 0), 7: (3, 1)}
+LAST = len(STEPS) - 1
+
+Y_REGIONS = [
+    [(0, CHUNK), (CHUNK, M)],
+    [(0, M)],
+    [(0, CHUNK), (CHUNK, 2 * CHUNK), (2 * CHUNK, M)],
+    [(0, CHUNK), (CHUNK, 2 * CHUNK), (2 * CHUNK, M - HALF), (M - HALF, M)],
+]
+MASK_REGIONS = [[(0, CHUNK), (CHUNK, M)], [(0, CHUNK), (CHUNK, M)], [(0, M)], [(0, M)]]
+WORD_REGIONS = [[(0, M)], [(0, M)], [(0, 2 * CHUNK), (2 * CHUNK, M)], [(0, CHUNK), (CHUNK, 2 * CHUNK), (2 * CHUNK, M)]]
+
+QUANTIZE_TOKENS_AT = {1: 1, 3: 2}
+INTERLEAVE_EXPAND_AT = {3: (2, 1), 5: (3, 0), 6: (3, 1)}
+QUANTIZE_EXPAND_AT = {4: [(2, 0), (2, 1)], 6: [(3, 0)], 7: [(3, 1)]}
+QUANTIZE_Y_AT = {2: [0], 3: [1], 5: [2], 6: [3], 7: [4], 8: [5], 9: [6, 7], 10: [8], 11: [9]}
 
 
 def tile_factorized_embedding_width_rows_g2_kernel(
@@ -67,7 +70,7 @@ def tile_factorized_embedding_width_rows_g2_kernel(
         ctx.enter_context(tc.manual_schedule())
 
         ident = keep.tile([P, P], F32, name="ident")
-        bias_rows = keep.tile([P, KP], BF16, name="bias_rows")
+        bias_rows = keep.tile([P, SPAN], BF16, name="bias_rows")
         bias_sb = keep.tile([P, 2, GROUPS, 2], BF16, name="bias_sb")
         x_codes = keep.tile([P, PASSES, M], U32, name="x_codes", align_bytes=64)
         x_scales = keep.tile([P, PASSES, M], U8, name="x_scales", align_bytes=64)
@@ -77,307 +80,258 @@ def tile_factorized_embedding_width_rows_g2_kernel(
         w_raw, w_grouped, w_codes, w_scales = {}, {}, {}, {}
         x_grouped, pos_sb, mask_sb, y_sb, y_words, y_grouped, acc = {}, {}, {}, {}, {}, {}, {}
 
-        def bias_of(g, t):
-            return bias_sb[:, t // 2, g, t % 2 : t % 2 + 1]
+        def span(c):
+            return slice(SPAN * c, SPAN * (c + 1))
 
-        def rows(g):
-            return slice(KP * g, KP * (g + 1))
-
-        def cols(n, lo=0, hi=NC):
-            return slice(NC * n + lo, NC * n + hi)
-
-        def load_first_w(g, c):
-            if (g, c) == (0, 0):
-                w_raw["first"] = keep.tile([P, 2, PASSES, PACK, KP], BF16, name="w_first", tag="w_raw")
-            w_raw[g, c] = w_raw["first"][:, g, c]
-            nc.sync.dma_start(out=w_raw[g, c], in_=expand[rows(c), rows(g)].rearrange("(p j) h -> p j h", j=PACK))
-
-        def load_last_w():
-            both = keep.tile([P, PASSES, PACK, 2 * KP], BF16, name="w_last", tag="w_raw")
-            for c in range(PASSES):
-                nc.sync.dma_start(
-                    out=both[:, c], in_=expand[rows(c), 2 * KP : 4 * KP].rearrange("(p j) h -> p j h", j=PACK)
-                )
-                for g in (2, 3):
-                    w_raw[g, c] = both[:, c, :, rows(g - 2)]
-
-        def load_x(h0, h1):
-            nc.sync.dma_start(
-                out=x_raw[:, 2 * h0 : 2 * h1, :].rearrange("p (h a) e -> p h (a e)", a=2),
-                in_=tokens[HALF * h0 : HALF * h1, :].rearrange("(h p a) e -> p h (a e)", p=P, a=2),
-            )
-
-        def load_pos(g):
-            pos_sb[g] = ring.tile([P, PACK, S], BF16, name="pos_sb", tag="pos_sb", bufs=4)
-            nc.sync.dma_start(out=pos_sb[g][:], in_=pos[rows(g), :].rearrange("(p t) s -> p t s", t=PACK))
+        def columns(k):
+            u, lo, hi, share = STEPS[k]
+            g, n = UNITS[u]
+            return g, CHUNK * n + lo, CHUNK * n + hi
 
         def window(tile, regions, m0, m1):
             r0, r1 = [r for r in regions if r[0] <= m0 < r[1]][0]
             return tile[:, PACK * r0 : PACK * r1].rearrange("p (t m) -> p t m", t=PACK)[:, :, m0 - r0 : m1 - r0]
 
-        def load_mask(g, r=0):
+        def load_tokens(h0, h1):
+            nc.sync.dma_start(
+                out=x_raw[:, 2 * h0 : 2 * h1, :].rearrange("p (h a) e -> p h (a e)", a=2),
+                in_=tokens[HALF * h0 : HALF * h1, :].rearrange("(h p a) e -> p h (a e)", p=P, a=2),
+            )
+
+        def load_expand(g, c):
+            w_raw[g, c] = ring.tile([P, PACK, SPAN], BF16, name="w_raw", tag="w_raw", bufs=2 * PASSES)
+            nc.sync.dma_start(out=w_raw[g, c][:], in_=expand[span(c), span(g)].rearrange("(p j) h -> p j h", j=PACK))
+
+        def load_pos(g):
+            pos_sb[g] = ring.tile([P, PACK, S], BF16, name="pos_sb", tag="pos_sb", bufs=GROUPS)
+            nc.sync.dma_start(out=pos_sb[g][:], in_=pos[span(g), :].rearrange("(p t) s -> p t s", t=PACK))
+
+        def load_mask(g, r):
             if r == 0:
-                mask_sb[g] = ring.tile([P, PACK * M], BF16, name="mask_sb", tag="mask_sb", bufs=4)
+                mask_sb[g] = ring.tile([P, PACK * M], BF16, name="mask_sb", tag="mask_sb", bufs=GROUPS)
             m0, m1 = MASK_REGIONS[g][r]
             nc.sync.dma_start(
                 out=window(mask_sb[g], MASK_REGIONS[g], m0, m1),
-                in_=mask_rows[rows(g), m0:m1].rearrange("(p t) m -> p t m", t=PACK),
+                in_=mask_rows[span(g), m0:m1].rearrange("(p t) m -> p t m", t=PACK),
             )
 
-        def group_w(g, c, copy, t0=0, t1=PACK):
+        def spread_bias():
+            bank = psum.tile([P, 2, P], F32, name="bias_bank", tag="bank0")
+            for u in range(2):
+                nc.tensor.transpose(bank[:, u, :], bias_rows[:].bitcast(F32)[:, u : SPAN // 2 : 2], ident[:])
+            nc.scalar.copy(
+                out=bias_sb[:].rearrange("p u g e -> p (u g e)").bitcast(F32).rearrange("p (u g) -> p u g", u=2),
+                in_=bank[:, :, 0:GROUPS],
+            )
+
+        def interleave_expand(g, c, copy, t0=0, t1=PACK):
             if (g, c) not in w_grouped:
-                w_grouped[g, c] = ring.tile([P, PACK * KP], BF16, name="w_grouped", tag="w_grouped", bufs=2, align_bytes=64)
-            dst = w_grouped[g, c][:].rearrange("p (t a e j) -> p a t e j", t=PACK, e=2, j=PACK)
-            src = w_raw[g, c].rearrange("p j (a e t) -> p a t e j", e=2, t=PACK)
+                w_grouped[g, c] = ring.tile([P, PACK * SPAN], BF16, name="w_grouped", tag="w_grouped", align_bytes=64)
+            dst = w_grouped[g, c][:].rearrange("p (t a d j) -> p a t d j", t=PACK, d=2, j=PACK)
+            src = w_raw[g, c][:].rearrange("p j (a d t) -> p a t d j", d=2, t=PACK)
             copy(out=dst[:, :, t0:t1], in_=src[:, :, t0:t1])
 
-        def quantize_w(g, c):
+        def quantize_expand(g, c):
             if c == 0:
-                w_codes[g] = ring.tile([P, PASSES, KP], U32, name="w_codes", tag="w_codes", bufs=2, align_bytes=64)
-                w_scales[g] = ring.tile([P, PASSES, KP], U8, name="w_scales", tag="w_scales", bufs=2, align_bytes=64)
+                w_codes[g] = ring.tile([P, PASSES, SPAN], U32, name="w_codes", tag="w_codes", bufs=2, align_bytes=64)
+                w_scales[g] = ring.tile([P, PASSES, SPAN], U8, name="w_scales", tag="w_scales", bufs=2, align_bytes=64)
             nc.vector.quantize_mx(
                 out=w_codes[g][:, c, :].bitcast(FP8X4), scales=w_scales[g][:, c, :], in_=w_grouped[g, c][:]
             )
 
-        def turn_x(n, c, h, bank_no):
+        def turn_tokens(n, c, h, bank_no):
             if h == 0:
-                x_grouped[n, c] = ring.tile([P, PACK * NC], BF16, name="x_grouped", tag="x_grouped", bufs=2, align_bytes=64)
+                x_grouped[n, c] = ring.tile(
+                    [P, PACK * CHUNK], BF16, name="x_grouped", tag="x_grouped", bufs=PASSES, align_bytes=64
+                )
             bank = psum.tile([P, 2, 2, P], F32, name="turned", tag="bank%d" % bank_no)
             for a in range(2):
-                words = x_raw[:, 4 * n + 2 * h + a, :].bitcast(F32)
+                words = x_raw[:, 2 * (2 * n + h) + a, :].bitcast(F32)
                 for u in range(2):
-                    nc.tensor.transpose(bank[:, a, u, :], words[:, 256 * c + u : 256 * (c + 1) : 2], ident[:])
-            dst = x_grouped[n, c][:].bitcast(F32)[:, 512 * h : 512 * (h + 1)]
+                    first = SPAN // 2 * c + u
+                    nc.tensor.transpose(bank[:, a, u, :], words[:, first : SPAN // 2 * (c + 1) : 2], ident[:])
+            dst = x_grouped[n, c][:].bitcast(F32)[:, 2 * HALF * h : 2 * HALF * (h + 1)]
             nc.scalar.copy(
                 out=dst.rearrange("p (r a u) -> p r a u", a=2, u=2), in_=bank[:].rearrange("p a u r -> p r a u")
             )
 
-        def turn_chunk(n):
-            for h in range(2):
-                for c in range(PASSES):
-                    turn_x(n, c, h, (2 * h + c) % 3)
-
-        def quantize_x(n, c, lo=0, hi=NC):
+        def quantize_tokens(n, c, lo=0, hi=CHUNK):
+            cols = slice(CHUNK * n + lo, CHUNK * n + hi)
             nc.vector.quantize_mx(
-                out=x_codes[:, c, cols(n, lo, hi)].bitcast(FP8X4),
-                scales=x_scales[:, c, cols(n, lo, hi)],
+                out=x_codes[:, c, cols].bitcast(FP8X4),
+                scales=x_scales[:, c, cols],
                 in_=x_grouped[n, c][:, PACK * lo : PACK * hi],
             )
 
         def multiply(u):
-            g, banks = UNITS[u]
-            for j, (t, n) in enumerate(banks):
-                acc[u, j] = psum.tile([P, NC], F32, name="acc", tag="bank%d" % (PACK * (u % 2) + j))
+            g, n = UNITS[u]
+            cols = slice(CHUNK * n, CHUNK * (n + 1))
+            for t in range(PACK):
+                acc[u, t] = psum.tile([P, CHUNK], F32, name="acc", tag="bank%d" % (PACK * (u % 2) + t))
                 for c in range(PASSES):
                     nc.tensor.matmul_mx(
-                        out=acc[u, j][:],
+                        out=acc[u, t][:],
                         lhsT=w_codes[g][:, c, P * t : P * (t + 1)].bitcast(FP8X4),
                         lhsT_scale=w_scales[g][:, c, P * t : P * (t + 1)],
-                        rhs=x_codes[:, c, cols(n)].bitcast(FP8X4),
-                        rhs_scale=x_scales[:, c, cols(n)],
+                        rhs=x_codes[:, c, cols].bitcast(FP8X4),
+                        rhs_scale=x_scales[:, c, cols],
                         start=(c == 0),
                         stop=(c == PASSES - 1),
                     )
 
-        def block_of_y(g, n, lo, hi):
-            return window(y_sb[g], Y_REGIONS[g], NC * n + lo, NC * n + hi)
-
-        def step_views(k):
+        def add_terms(k, t, a, b):
             u, lo, hi, share = STEPS[k]
-            g, banks = UNITS[u]
-            if g == 7:
-                s = u - 6
-                flat = slice(PACK * NC * s, PACK * NC * (s + 1))
-                y_part = y_sb[g][:, flat].rearrange("p (j m) -> p j m", j=PACK)
-                mask_part = mask_sb[g][:, flat].rearrange("p (j m) -> p j m", j=PACK)
-                return y_part, mask_part
-            n = banks[0][1]
-            return block_of_y(g, n, lo, hi), window(mask_sb[g], MASK_REGIONS[g], NC * n + lo, NC * n + hi)
-
-        def add_terms(k, j, a, b):
-            u, lo, hi, share = STEPS[k]
-            g, banks = UNITS[u]
+            g, m0, m1 = columns(k)
             if g not in y_sb:
                 y_sb[g] = ring.tile([P, PACK * M], F32, name="y_sb", tag="big")
-            y_part, mask_part = step_views(k)
-            t, n = banks[j]
-            first = (NC * n) % S + lo
-            wrap = S - first
-            for c0, c1 in ([(a, wrap), (wrap, b)] if a < wrap < b else [(a, b)]):
-                i0 = (first + c0) % S
+            wrap = S - m0 % S
+            for c0, c1 in [(a, wrap), (wrap, b)] if a < wrap < b else [(a, b)]:
+                i0 = (m0 + c0) % S
                 nc.vector.scalar_tensor_tensor(
-                    out=y_part[:, j, c0:c1],
-                    in0=acc[u, j][:, lo + c0 : lo + c1],
-                    scalar=bias_of(g, t),
+                    out=window(y_sb[g], Y_REGIONS[g], m0, m1)[:, t, c0:c1],
+                    in0=acc[u, t][:, lo + c0 : lo + c1],
+                    scalar=bias_sb[:, t // 2, g, t % 2 : t % 2 + 1],
                     in1=pos_sb[g][:, t, i0 : i0 + c1 - c0],
                     op0=ADD,
                     op1=ADD,
                 )
 
-        def apply_mask(engine, k, j0, j1, a, b):
-            y_part, mask_part = step_views(k)
-            engine.tensor_tensor(
-                out=y_part[:, j0:j1, a:b], in0=y_part[:, j0:j1, a:b], in1=mask_part[:, j0:j1, a:b], op=MULT
-            )
+        def apply_mask(engine, k, t0, t1, a, b):
+            g, m0, m1 = columns(k)
+            part = window(y_sb[g], Y_REGIONS[g], m0, m1)[:, t0:t1, a:b]
+            factor = window(mask_sb[g], MASK_REGIONS[g], m0, m1)[:, t0:t1, a:b]
+            engine.tensor_tensor(out=part, in0=part, in1=factor, op=MULT)
 
-        def group_y(i, copy):
-            g, n, lo, hi = BLOCKS[i]
-            y_grouped[i] = ring.tile(
-                [P, PACK * (hi - lo)], BF16, name="y_grouped", tag="y_grouped", bufs=3, align_bytes=64
+        def interleave_y(k, copy):
+            g, m0, m1 = columns(k)
+            y_grouped[k] = ring.tile(
+                [P, PACK * (m1 - m0)], BF16, name="y_grouped", tag="y_grouped", bufs=4, align_bytes=64
             )
             copy(
-                out=y_grouped[i][:].rearrange("p (c i t) -> p c t i", i=4, t=PACK),
-                in_=block_of_y(g, n, lo, hi).rearrange("p t (c i) -> p c t i", i=4),
+                out=y_grouped[k][:].rearrange("p (c i t) -> p c t i", i=4, t=PACK),
+                in_=window(y_sb[g], Y_REGIONS[g], m0, m1).rearrange("p t (c i) -> p c t i", i=4),
             )
 
-        def quantize_y(i):
-            g, n, lo, hi = BLOCKS[i]
+        def quantize_y(k):
+            g, m0, m1 = columns(k)
             if g not in y_words:
-                y_words[g] = ring.tile([P, M], U32, name="y_words", tag="y_words", bufs=3, align_bytes=64)
+                y_words[g] = ring.tile([P, M], U32, name="y_words", tag="y_words", align_bytes=64)
             nc.vector.quantize_mx(
-                out=y_words[g][:, cols(n, lo, hi)].bitcast(FP8X4),
-                scales=y_scales[PACK * g : P, cols(n, lo, hi)],
-                in_=y_grouped[i][:],
+                out=y_words[g][:, m0:m1].bitcast(FP8X4), scales=y_scales[PACK * g : P, m0:m1], in_=y_grouped[k][:]
             )
 
-        def store_y_flat(g, f0, f1):
-            nc.sync.dma_start(
-                out=y_rows[rows(g), :].rearrange("(p t) m -> p (t m)", t=PACK)[:, f0:f1], in_=y_sb[g][:, f0:f1]
-            )
+        def store_y(k):
+            g, m0, m1 = columns(k)
+            for r0, r1 in Y_REGIONS[g]:
+                if r1 == m1:
+                    nc.sync.dma_start(
+                        out=y_rows[span(g), r0:r1].rearrange("(p t) m -> p t m", t=PACK),
+                        in_=window(y_sb[g], Y_REGIONS[g], r0, r1),
+                    )
 
-        def store_y_region(g, r):
-            m0, m1 = Y_REGIONS[g][r]
-            nc.sync.dma_start(
-                out=y_rows[rows(g), m0:m1].rearrange("(p t) m -> p t m", t=PACK),
-                in_=window(y_sb[g], Y_REGIONS[g], m0, m1),
-            )
-
-        def store_after(k):
-            if k in Y_STORE_AFTER:
-                store_y_region(*Y_STORE_AFTER[k])
-
-        def store_words(g, m0, m1):
-            nc.sync.dma_start(out=words_out[g, :, m0:m1], in_=y_words[g][:, m0:m1].bitcast(I32))
-
-        def store_scales(q):
-            nc.scalar.dma_start(
-                out=scales_out[:, 4 * q : 4 * q + 4, :], in_=y_scales[32 * q : 32 * q + 16, :].bitcast(I32)
-            )
+        def store_words(k):
+            g, m0, m1 = columns(k)
+            for r0, r1 in WORD_REGIONS[g]:
+                if r1 == m1:
+                    nc.sync.dma_start(out=words_out[g, :, r0:r1], in_=y_words[g][:, r0:r1].bitcast(I32))
 
         nc.vector.memset(bias_rows[:], 0.0)
         make_identity(nc, ident[:])
-        load_x(0, 1)
+        load_tokens(0, 1)
         nc.sync.dma_start(out=bias_rows[0:GROUPS, :], in_=bias.rearrange("(g h) -> g h", g=GROUPS))
-        load_first_w(0, 0)
-        load_x(1, 2)
-        load_first_w(0, 1)
+        load_expand(0, 0)
+        load_tokens(1, 2)
+        load_expand(0, 1)
         load_pos(0)
-        load_first_w(1, 0)
-        load_first_w(1, 1)
-        load_x(2, 3)
+        load_expand(1, 0)
+        load_expand(1, 1)
+        load_tokens(2, 3)
         load_pos(1)
         load_mask(0, 0)
-        load_x(3, 4)
+
+        turn_tokens(0, 0, 0, 4)
+        turn_tokens(0, 1, 0, 5)
+        interleave_expand(0, 0, nc.vector.tensor_copy)
+        quantize_tokens(0, 0, 0, HALF)
+        quantize_expand(0, 0)
+        quantize_tokens(0, 1, 0, HALF)
+        turn_tokens(0, 0, 1, 6)
+        turn_tokens(0, 1, 1, 7)
+        spread_bias()
+        interleave_expand(0, 1, nc.vector.tensor_copy)
+        quantize_tokens(0, 0, HALF, CHUNK)
+        quantize_expand(0, 1)
+        quantize_tokens(0, 1, HALF, CHUNK)
+        multiply(0)
+        load_expand(2, 0)
+        load_tokens(3, 4)
         load_mask(1, 0)
         load_mask(0, 1)
-        load_x(4, 6)
+        load_tokens(4, 6)
+        load_expand(2, 1)
+        load_mask(1, 1)
+        interleave_expand(1, 0, nc.scalar.copy)
+        interleave_expand(1, 1, nc.scalar.copy, 0, PACK // 2)
 
-        turn_x(0, 0, 0, 4)
-        turn_x(0, 1, 0, 5)
-        group_w(0, 0, nc.vector.tensor_copy)
-        quantize_x(0, 0, 0, HALF)
-        quantize_w(0, 0)
-        quantize_x(0, 1, 0, HALF)
-        turn_x(0, 0, 1, 6)
-        turn_x(0, 1, 1, 7)
-        bias_bank = psum.tile([P, 2, P], F32, name="bias_bank", tag="bank0")
-        for u in range(2):
-            nc.tensor.transpose(bias_bank[:, u, :], bias_rows[:].bitcast(F32)[:, u : KP // 2 : 2], ident[:])
-        nc.scalar.copy(
-            out=bias_sb[:].rearrange("p u g e -> p (u g e)").bitcast(F32).rearrange("p (u g) -> p u g", u=2),
-            in_=bias_bank[:, :, 0:GROUPS],
-        )
-        group_w(0, 1, nc.vector.tensor_copy)
-        quantize_x(0, 0, HALF, NC)
-        quantize_w(0, 1)
-        quantize_x(0, 1, HALF, NC)
-        multiply(0)
-        group_w(1, 0, nc.scalar.copy)
-        group_w(1, 1, nc.scalar.copy, 0, W_SPLIT)
-
-        last = len(STEPS) - 1
-        for k in range(last + 1):
+        for k in range(LAST + 1):
             u, lo, hi, share = STEPS[k]
             width = hi - lo
-            if k > 0 and STEPS[k - 1][3]:
-                before = STEPS[k - 1][2] - STEPS[k - 1][1]
-                add_terms(k - 1, PACK - 1, before - HELD, before)
-                apply_mask(nc.gpsimd, k - 1, 0, PACK, before - STEPS[k - 1][3], before)
-                store_after(k - 1)
-            for j in range(PACK - 1):
-                add_terms(k, j, 0, width)
-            add_terms(k, PACK - 1, 0, width - HELD if share else width)
 
-            if k in (6, 7):
-                group_w(*GROUP_W_AT[k], nc.scalar.copy)
-            for i in GROUP_Y_AT.get(k, []):
-                group_y(i, nc.scalar.copy)
-            if k in (3, 4):
-                group_w(*GROUP_W_AT[k], nc.scalar.copy)
+            for t in range(PACK - 1):
+                add_terms(k, t, 0, width)
+            add_terms(k, PACK - 1, 0, width - HELD if k < LAST else width)
+
+            if k in INTERLEAVE_EXPAND_AT:
+                interleave_expand(*INTERLEAVE_EXPAND_AT[k], nc.scalar.copy)
+            if k > 0:
+                interleave_y(k - 1, nc.scalar.copy)
 
             if k == 0:
-                group_w(1, 1, nc.vector.tensor_copy, W_SPLIT)
-                quantize_w(1, 0)
-                load_last_w()
-                load_pos(2)
-                load_mask(2)
-                load_pos(3)
-                load_mask(3)
-            if k in (1, 3):
-                quantize_x(k // 2 + 1, 0)
-                quantize_x(k // 2 + 1, 1)
-            if k in (5, 8):
-                quantize_w(*GROUP_W_AT[k - 1])
-            if k == 0:
-                quantize_w(1, 1)
-                turn_x(1, 0, 0, 0)
-                turn_x(1, 1, 0, 1)
-            if lo == 0 and u + 1 < len(UNITS):
+                interleave_expand(1, 1, nc.vector.tensor_copy, PACK // 2)
+                quantize_expand(1, 0)
+                load_expand(3, 0)
+                load_expand(3, 1)
+                for g in (2, 3):
+                    load_pos(g)
+                    load_mask(g, 0)
+                quantize_expand(1, 1)
+                turn_tokens(1, 0, 0, 0)
+                turn_tokens(1, 1, 0, 1)
+                interleave_expand(2, 0, nc.scalar.copy)
+            if k in QUANTIZE_TOKENS_AT:
+                for c in range(PASSES):
+                    quantize_tokens(QUANTIZE_TOKENS_AT[k], c)
+            if u + 1 < len(UNITS):
                 multiply(u + 1)
             if k == 0:
-                turn_x(1, 0, 1, 2)
-                turn_x(1, 1, 1, 0)
+                turn_tokens(1, 0, 1, 2)
+                turn_tokens(1, 1, 1, 0)
             if k == 2:
-                turn_chunk(2)
-            if k in (3, 5, 8):
-                apply_mask(nc.vector, k, 0, PACK, 0, width - share)
-                quantize_y(k - 2)
-            elif k in (4, 7):
-                quantize_y(k - 2)
-                apply_mask(nc.vector, k, 0, PACK, 0, width - share)
-                quantize_w(*GROUP_W_AT[k - 1])
-            else:
-                if k >= 2:
-                    quantize_y(k - 2)
-                apply_mask(nc.vector, k, 2, PACK, 0, width - share)
-                apply_mask(nc.vector, k, 0, 2, 0, width - share)
-            if k == 6:
-                store_words(0, 0, M)
-            if k == 7:
-                store_words(1, 0, M)
-            if k == 9:
-                store_words(2, 0, 2 * NC)
-            if k == 10:
-                store_words(2, 2 * NC, M)
-            if k == 11:
-                store_words(3, 0, NC)
-            if k == 12:
-                store_words(3, NC, 2 * NC)
+                for h in range(2):
+                    for c in range(PASSES):
+                        turn_tokens(2, c, h, (2 * h + c) % 3)
 
-        store_after(last)
-        quantize_y(11)
-        group_y(12, nc.vector.tensor_copy)
-        quantize_y(12)
-        store_words(3, 2 * NC, M)
-        for q in range(4):
-            store_scales(q)
+            if k < LAST:
+                for g, c in QUANTIZE_EXPAND_AT.get(k, []):
+                    quantize_expand(g, c)
+                for i in QUANTIZE_Y_AT.get(k, []):
+                    quantize_y(i)
+                    store_words(i)
+                add_terms(k, PACK - 1, width - HELD, width)
+                apply_mask(nc.vector, k, 0, PACK, 0, width - share)
+                apply_mask(nc.gpsimd, k, 0, PACK, width - share, width)
+                store_y(k)
+
+        apply_mask(nc.vector, LAST, 0, PACK // 2, 0, HALF)
+        apply_mask(nc.vector, LAST, PACK // 2, PACK, 0, HALF)
+        store_y(LAST)
+        interleave_y(LAST, nc.vector.tensor_copy)
+        for i in range(LAST - 2, LAST + 1):
+            quantize_y(i)
+            store_words(i)
+
+        for q in range(P // QUADRANT):
+            nc.scalar.dma_start(
+                out=scales_out[:, PACK * q : PACK * (q + 1), :],
+                in_=y_scales[QUADRANT * q : QUADRANT * q + PACK * GROUPS, :].bitcast(I32),
+            )

from contextlib import ExitStack

import concourse.mybir as mybir
from concourse.masks import make_identity

B, S, E, H = 4, 384, 1024, 2048
M = B * S
FLOPS = 2 * M * E * H

F32 = mybir.dt.float32
BF16 = mybir.dt.bfloat16
I32 = mybir.dt.int32
U32 = mybir.dt.uint32
U8 = mybir.dt.uint8
FP8X4 = mybir.dt.float8_e4m3fn_x4
ADD = mybir.AluOpType.add
MULT = mybir.AluOpType.mult

P = 128
PACK = 4
SPAN = P * PACK
PASSES = E // SPAN
GROUPS = H // SPAN
CHUNK = 512
CHUNKS = M // CHUNK
HALF = CHUNK // 2
QUADRANT = 32

SHARE = 216
SHORT_SHARE = 96
HELD = 64

UNITS = [(g, n) for n in range(CHUNKS) for g in (0, 1)] + [(g, n) for g in (2, 3) for n in range(CHUNKS)]
STEPS = (
    [(u, 0, CHUNK, SHARE) for u in range(len(UNITS) - 2)]
    + [(len(UNITS) - 2, 0, CHUNK, SHORT_SHARE)]
    + [(len(UNITS) - 1, 0, HALF, SHORT_SHARE), (len(UNITS) - 1, HALF, CHUNK, 0)]
)
LAST = len(STEPS) - 1

Y_REGIONS = [
    [(0, CHUNK), (CHUNK, M)],
    [(0, M)],
    [(0, CHUNK), (CHUNK, 2 * CHUNK), (2 * CHUNK, M)],
    [(0, CHUNK), (CHUNK, 2 * CHUNK), (2 * CHUNK, M - HALF), (M - HALF, M)],
]
MASK_REGIONS = [[(0, CHUNK), (CHUNK, M)], [(0, CHUNK), (CHUNK, M)], [(0, M)], [(0, M)]]
WORD_REGIONS = [[(0, M)], [(0, M)], [(0, 2 * CHUNK), (2 * CHUNK, M)], [(0, CHUNK), (CHUNK, 2 * CHUNK), (2 * CHUNK, M)]]

QUANTIZE_TOKENS_AT = {1: 1, 3: 2}
INTERLEAVE_EXPAND_AT = {3: (2, 1), 5: (3, 0), 6: (3, 1)}
QUANTIZE_EXPAND_AT = {4: [(2, 0), (2, 1)], 6: [(3, 0)], 7: [(3, 1)]}
QUANTIZE_Y_AT = {2: [0], 3: [1], 5: [2], 6: [3], 7: [4], 8: [5], 9: [6, 7], 10: [8], 11: [9]}


def tile_factorized_embedding_width_rows_g2_kernel(
    tc, token_rows, expand, bias, pos, mask, out_0, out_1, out_2
):
    nc = tc.nc
    tokens = token_rows.rearrange("b s e -> (b s) e")
    mask_rows = mask.rearrange("h b s -> h (b s)")
    y_rows = out_0.rearrange("h b s -> h (b s)")
    words_out = out_1.rearrange("g p m t -> g p (m t)").bitcast(I32)
    scales_out = out_2.bitcast(I32)

    with ExitStack() as ctx:
        keep = ctx.enter_context(tc.tile_pool(name="keep", bufs=1))
        ring = ctx.enter_context(tc.tile_pool(name="ring", bufs=3))
        psum = ctx.enter_context(tc.psum_pool(name="psum", bufs=1))
        ctx.enter_context(tc.manual_schedule())

        ident = keep.tile([P, P], F32, name="ident")
        bias_rows = keep.tile([P, SPAN], BF16, name="bias_rows")
        bias_sb = keep.tile([P, 2, GROUPS, 2], BF16, name="bias_sb")
        x_codes = keep.tile([P, PASSES, M], U32, name="x_codes", align_bytes=64)
        x_scales = keep.tile([P, PASSES, M], U8, name="x_scales", align_bytes=64)
        y_scales = keep.tile([P, M], U8, name="y_scales", align_bytes=64)
        x_raw = ring.tile([P, M // P, E], BF16, name="x_raw", tag="big")

        w_raw, w_grouped, w_codes, w_scales = {}, {}, {}, {}
        x_grouped, pos_sb, mask_sb, y_sb, y_words, y_grouped, acc = {}, {}, {}, {}, {}, {}, {}

        def span(c):
            return slice(SPAN * c, SPAN * (c + 1))

        def columns(k):
            u, lo, hi, share = STEPS[k]
            g, n = UNITS[u]
            return g, CHUNK * n + lo, CHUNK * n + hi

        def window(tile, regions, m0, m1):
            r0, r1 = [r for r in regions if r[0] <= m0 < r[1]][0]
            return tile[:, PACK * r0 : PACK * r1].rearrange("p (t m) -> p t m", t=PACK)[:, :, m0 - r0 : m1 - r0]

        def load_tokens(h0, h1):
            nc.sync.dma_start(
                out=x_raw[:, 2 * h0 : 2 * h1, :].rearrange("p (h a) e -> p h (a e)", a=2),
                in_=tokens[HALF * h0 : HALF * h1, :].rearrange("(h p a) e -> p h (a e)", p=P, a=2),
            )

        def load_expand(g, c):
            w_raw[g, c] = ring.tile([P, PACK, SPAN], BF16, name="w_raw", tag="w_raw", bufs=2 * PASSES)
            nc.sync.dma_start(out=w_raw[g, c][:], in_=expand[span(c), span(g)].rearrange("(p j) h -> p j h", j=PACK))

        def load_pos(g):
            pos_sb[g] = ring.tile([P, PACK, S], BF16, name="pos_sb", tag="pos_sb", bufs=GROUPS)
            nc.sync.dma_start(out=pos_sb[g][:], in_=pos[span(g), :].rearrange("(p t) s -> p t s", t=PACK))

        def load_mask(g, r):
            if r == 0:
                mask_sb[g] = ring.tile([P, PACK * M], BF16, name="mask_sb", tag="mask_sb", bufs=GROUPS)
            m0, m1 = MASK_REGIONS[g][r]
            nc.sync.dma_start(
                out=window(mask_sb[g], MASK_REGIONS[g], m0, m1),
                in_=mask_rows[span(g), m0:m1].rearrange("(p t) m -> p t m", t=PACK),
            )

        def spread_bias():
            bank = psum.tile([P, 2, P], F32, name="bias_bank", tag="bank0")
            for u in range(2):
                nc.tensor.transpose(bank[:, u, :], bias_rows[:].bitcast(F32)[:, u : SPAN // 2 : 2], ident[:])
            nc.scalar.copy(
                out=bias_sb[:].rearrange("p u g e -> p (u g e)").bitcast(F32).rearrange("p (u g) -> p u g", u=2),
                in_=bank[:, :, 0:GROUPS],
            )

        def interleave_expand(g, c, copy, t0=0, t1=PACK):
            if (g, c) not in w_grouped:
                w_grouped[g, c] = ring.tile([P, PACK * SPAN], BF16, name="w_grouped", tag="w_grouped", align_bytes=64)
            dst = w_grouped[g, c][:].rearrange("p (t a d j) -> p a t d j", t=PACK, d=2, j=PACK)
            src = w_raw[g, c][:].rearrange("p j (a d t) -> p a t d j", d=2, t=PACK)
            copy(out=dst[:, :, t0:t1], in_=src[:, :, t0:t1])

        def quantize_expand(g, c):
            if c == 0:
                w_codes[g] = ring.tile([P, PASSES, SPAN], U32, name="w_codes", tag="w_codes", bufs=2, align_bytes=64)
                w_scales[g] = ring.tile([P, PASSES, SPAN], U8, name="w_scales", tag="w_scales", bufs=2, align_bytes=64)
            nc.vector.quantize_mx(
                out=w_codes[g][:, c, :].bitcast(FP8X4), scales=w_scales[g][:, c, :], in_=w_grouped[g, c][:]
            )

        def turn_tokens(n, c, h, bank_no):
            if h == 0:
                x_grouped[n, c] = ring.tile(
                    [P, PACK * CHUNK], BF16, name="x_grouped", tag="x_grouped", bufs=PASSES, align_bytes=64
                )
            bank = psum.tile([P, 2, 2, P], F32, name="turned", tag="bank%d" % bank_no)
            for a in range(2):
                words = x_raw[:, 2 * (2 * n + h) + a, :].bitcast(F32)
                for u in range(2):
                    first = SPAN // 2 * c + u
                    nc.tensor.transpose(bank[:, a, u, :], words[:, first : SPAN // 2 * (c + 1) : 2], ident[:])
            dst = x_grouped[n, c][:].bitcast(F32)[:, 2 * HALF * h : 2 * HALF * (h + 1)]
            nc.scalar.copy(
                out=dst.rearrange("p (r a u) -> p r a u", a=2, u=2), in_=bank[:].rearrange("p a u r -> p r a u")
            )

        def quantize_tokens(n, c, lo=0, hi=CHUNK):
            cols = slice(CHUNK * n + lo, CHUNK * n + hi)
            nc.vector.quantize_mx(
                out=x_codes[:, c, cols].bitcast(FP8X4),
                scales=x_scales[:, c, cols],
                in_=x_grouped[n, c][:, PACK * lo : PACK * hi],
            )

        def multiply(u):
            g, n = UNITS[u]
            cols = slice(CHUNK * n, CHUNK * (n + 1))
            for t in range(PACK):
                acc[u, t] = psum.tile([P, CHUNK], F32, name="acc", tag="bank%d" % (PACK * (u % 2) + t))
                for c in range(PASSES):
                    nc.tensor.matmul_mx(
                        out=acc[u, t][:],
                        lhsT=w_codes[g][:, c, P * t : P * (t + 1)].bitcast(FP8X4),
                        lhsT_scale=w_scales[g][:, c, P * t : P * (t + 1)],
                        rhs=x_codes[:, c, cols].bitcast(FP8X4),
                        rhs_scale=x_scales[:, c, cols],
                        start=(c == 0),
                        stop=(c == PASSES - 1),
                    )

        def add_terms(k, t, a, b):
            u, lo, hi, share = STEPS[k]
            g, m0, m1 = columns(k)
            if g not in y_sb:
                y_sb[g] = ring.tile([P, PACK * M], F32, name="y_sb", tag="big")
            wrap = S - m0 % S
            for c0, c1 in [(a, wrap), (wrap, b)] if a < wrap < b else [(a, b)]:
                i0 = (m0 + c0) % S
                nc.vector.scalar_tensor_tensor(
                    out=window(y_sb[g], Y_REGIONS[g], m0, m1)[:, t, c0:c1],
                    in0=acc[u, t][:, lo + c0 : lo + c1],
                    scalar=bias_sb[:, t // 2, g, t % 2 : t % 2 + 1],
                    in1=pos_sb[g][:, t, i0 : i0 + c1 - c0],
                    op0=ADD,
                    op1=ADD,
                )

        def apply_mask(engine, k, t0, t1, a, b):
            g, m0, m1 = columns(k)
            part = window(y_sb[g], Y_REGIONS[g], m0, m1)[:, t0:t1, a:b]
            factor = window(mask_sb[g], MASK_REGIONS[g], m0, m1)[:, t0:t1, a:b]
            engine.tensor_tensor(out=part, in0=part, in1=factor, op=MULT)

        def interleave_y(k, copy):
            g, m0, m1 = columns(k)
            y_grouped[k] = ring.tile(
                [P, PACK * (m1 - m0)], BF16, name="y_grouped", tag="y_grouped", bufs=4, align_bytes=64
            )
            copy(
                out=y_grouped[k][:].rearrange("p (c i t) -> p c t i", i=4, t=PACK),
                in_=window(y_sb[g], Y_REGIONS[g], m0, m1).rearrange("p t (c i) -> p c t i", i=4),
            )

        def quantize_y(k):
            g, m0, m1 = columns(k)
            if g not in y_words:
                y_words[g] = ring.tile([P, M], U32, name="y_words", tag="y_words", align_bytes=64)
            nc.vector.quantize_mx(
                out=y_words[g][:, m0:m1].bitcast(FP8X4), scales=y_scales[PACK * g : P, m0:m1], in_=y_grouped[k][:]
            )

        def store_y(k):
            g, m0, m1 = columns(k)
            for r0, r1 in Y_REGIONS[g]:
                if r1 == m1:
                    nc.sync.dma_start(
                        out=y_rows[span(g), r0:r1].rearrange("(p t) m -> p t m", t=PACK),
                        in_=window(y_sb[g], Y_REGIONS[g], r0, r1),
                    )

        def store_words(k):
            g, m0, m1 = columns(k)
            for r0, r1 in WORD_REGIONS[g]:
                if r1 == m1:
                    nc.sync.dma_start(out=words_out[g, :, r0:r1], in_=y_words[g][:, r0:r1].bitcast(I32))

        nc.vector.memset(bias_rows[:], 0.0)
        make_identity(nc, ident[:])
        load_tokens(0, 1)
        nc.sync.dma_start(out=bias_rows[0:GROUPS, :], in_=bias.rearrange("(g h) -> g h", g=GROUPS))
        load_expand(0, 0)
        load_tokens(1, 2)
        load_expand(0, 1)
        load_pos(0)
        load_expand(1, 0)
        load_expand(1, 1)
        load_tokens(2, 3)
        load_pos(1)
        load_mask(0, 0)

        turn_tokens(0, 0, 0, 4)
        turn_tokens(0, 1, 0, 5)
        interleave_expand(0, 0, nc.vector.tensor_copy)
        quantize_tokens(0, 0, 0, HALF)
        quantize_expand(0, 0)
        quantize_tokens(0, 1, 0, HALF)
        turn_tokens(0, 0, 1, 6)
        turn_tokens(0, 1, 1, 7)
        spread_bias()
        interleave_expand(0, 1, nc.vector.tensor_copy)
        quantize_tokens(0, 0, HALF, CHUNK)
        quantize_expand(0, 1)
        quantize_tokens(0, 1, HALF, CHUNK)
        multiply(0)
        load_expand(2, 0)
        load_tokens(3, 4)
        load_mask(1, 0)
        load_mask(0, 1)
        load_tokens(4, 6)
        load_expand(2, 1)
        load_mask(1, 1)
        interleave_expand(1, 0, nc.scalar.copy)
        interleave_expand(1, 1, nc.scalar.copy, 0, PACK // 2)

        for k in range(LAST + 1):
            u, lo, hi, share = STEPS[k]
            width = hi - lo

            for t in range(PACK - 1):
                add_terms(k, t, 0, width)
            add_terms(k, PACK - 1, 0, width - HELD if k < LAST else width)

            if k in INTERLEAVE_EXPAND_AT:
                interleave_expand(*INTERLEAVE_EXPAND_AT[k], nc.scalar.copy)
            if k > 0:
                interleave_y(k - 1, nc.scalar.copy)

            if k == 0:
                interleave_expand(1, 1, nc.vector.tensor_copy, PACK // 2)
                quantize_expand(1, 0)
                load_expand(3, 0)
                load_expand(3, 1)
                for g in (2, 3):
                    load_pos(g)
                    load_mask(g, 0)
                quantize_expand(1, 1)
                turn_tokens(1, 0, 0, 0)
                turn_tokens(1, 1, 0, 1)
                interleave_expand(2, 0, nc.scalar.copy)
            if k in QUANTIZE_TOKENS_AT:
                for c in range(PASSES):
                    quantize_tokens(QUANTIZE_TOKENS_AT[k], c)
            if u + 1 < len(UNITS):
                multiply(u + 1)
            if k == 0:
                turn_tokens(1, 0, 1, 2)
                turn_tokens(1, 1, 1, 0)
            if k == 2:
                for h in range(2):
                    for c in range(PASSES):
                        turn_tokens(2, c, h, (2 * h + c) % 3)

            if k < LAST:
                for g, c in QUANTIZE_EXPAND_AT.get(k, []):
                    quantize_expand(g, c)
                for i in QUANTIZE_Y_AT.get(k, []):
                    quantize_y(i)
                    store_words(i)
                add_terms(k, PACK - 1, width - HELD, width)
                apply_mask(nc.vector, k, 0, PACK, 0, width - share)
                apply_mask(nc.gpsimd, k, 0, PACK, width - share, width)
                store_y(k)

        apply_mask(nc.vector, LAST, 0, PACK // 2, 0, HALF)
        apply_mask(nc.vector, LAST, PACK // 2, PACK, 0, HALF)
        store_y(LAST)
        interleave_y(LAST, nc.vector.tensor_copy)
        for i in range(LAST - 2, LAST + 1):
            quantize_y(i)
            store_words(i)

        for q in range(P // QUADRANT):
            nc.scalar.dma_start(
                out=scales_out[:, PACK * q : PACK * (q + 1), :],
                in_=y_scales[QUADRANT * q : QUADRANT * q + PACK * GROUPS, :].bitcast(I32),
            )
